import numpy as np
import ml_dtypes


def mxq(x, axis, fmt="e4m3"):
    dtype, down = {"e4m3": (ml_dtypes.float8_e4m3fn, 7), "e5m2": (ml_dtypes.float8_e5m2, 14)}[fmt]
    v = np.moveaxis(np.asarray(x, np.float32).astype(ml_dtypes.bfloat16).astype(np.float64), axis, -1)
    blocks = v.reshape(v.shape[:-1] + (-1, 32))
    amax = np.abs(blocks).max(-1, keepdims=True)
    byte = np.maximum(np.where(amax > 0, np.frexp(amax)[1] - 1 + 127, 0) - down, 1)
    scale = np.exp2(byte - 127.0)
    codes = (blocks / scale).astype(np.float32).astype(dtype).astype(np.float64)
    return np.moveaxis((codes * scale).reshape(v.shape), -1, axis)


WIDE = False


def mx_kscale(k):
    if not WIDE:
        return np.ones(k)
    levels = np.array([30, -30])
    if k % 512:
        return np.exp2(np.random.permutation(np.resize(levels, k // 32))).repeat(32)
    a = np.empty((k // 512, 16))
    for p in range(k // 512):
        a[p, :8] = np.random.permutation(np.resize(levels, 8))
        for g in range(8):
            far = levels[np.abs(levels - a[p, g]) >= 10]
            a[p, g + 8] = far[np.random.randint(len(far))]
    return np.exp2(a.ravel()).repeat(32)


def f64(x):
    return np.asarray(x).astype(np.float64)


def striped(idx):
    return np.tile(np.asarray(idx).reshape(-1, 16).T, (8, 1)).astype(np.uint16)


def unstriped(offs):
    return offs[:16].T.reshape(-1).astype(np.int64)


E2M1 = np.array([0.0, 0.5, 1.0, 1.5, 2.0, 3.0, 4.0, 6.0, -0.0, -0.5, -1.0, -1.5, -2.0, -3.0, -4.0, -6.0])


def pack_weight(w, fmt):
    k, n = w.shape
    w = f64(np.asarray(w, np.float32).astype(ml_dtypes.bfloat16)).reshape(k // 32, 32, n)
    amax = np.abs(w).max(1)
    if fmt in ("e4m3", "e5m2"):
        byte = np.frexp(amax)[1] - 1 + 127 - (7 if fmt == "e4m3" else 14)
    else:
        mant, ex = np.frexp(amax / 6.0)
        byte = np.where(mant > 0.5, ex, ex - 1) + 127
    byte = np.clip(np.where(amax > 0, byte, 1), 1, 254)
    scaled = (w * np.exp2(127.0 - byte)[:, None, :]).reshape(k, n).astype(np.float32)
    by_word = np.ascontiguousarray(scaled.reshape(k // 512, 128, 4, n).transpose(0, 1, 3, 2))
    if fmt in ("e4m3", "e5m2"):
        words = by_word.astype(ml_dtypes.float8_e4m3fn if fmt == "e4m3" else ml_dtypes.float8_e5m2).view(np.uint8)
    else:
        c = by_word.astype(ml_dtypes.float4_e2m1fn).view(np.uint8) & 0xF
        words = (c[..., 0::2] | (c[..., 1::2] << 4)).reshape(k // 512, 128, 2 * n)
    return np.ascontiguousarray(words), np.ascontiguousarray(byte.astype(np.uint8).reshape(k // 512, 16, n))


def unpack_weight(words, scales, fmt):
    g, _, n = scales.shape
    words = np.ascontiguousarray(words).reshape(g, 128, n, -1)
    if fmt in ("e4m3", "e5m2"):
        vals = words.view(ml_dtypes.float8_e4m3fn if fmt == "e4m3" else ml_dtypes.float8_e5m2).astype(np.float64)
    else:
        nib = np.empty((g, 128, n, 4), np.uint8)
        nib[..., 0::2] = words & 0xF
        nib[..., 1::2] = words >> 4
        vals = E2M1[nib]
    vals = vals * np.repeat(np.exp2(scales.astype(np.float64) - 127.0), 8, axis=1)[..., None]
    return vals.transpose(0, 1, 3, 2).reshape(g * 512, n)


K, T, J, R, C, O, N = 512, 1024, 256, 512, 512, 128, 256


def setup_inputs():
    n = np.random.standard_normal
    idx = np.random.permutation(T)[:J]
    idx2 = np.random.permutation(C)[:J]
    idx3 = np.random.permutation(C)[:O]
    idx4 = np.random.permutation(J)[:O]
    idx5 = np.random.permutation(T)[:O]
    fk = mx_kscale(K)
    fr = mx_kscale(R)
    xtp = pack_weight(n((K, T)) / fk[:, None], "e2m1")
    wp = pack_weight(n((K, R)) * 1 / np.sqrt(K) * fk[:, None] * fr, "e4m3")
    w2p = pack_weight(n((K, R)) * 1 / np.sqrt(K) * fk[:, None] * fr, "e5m2")
    wbp = pack_weight(n((R, N)) * 1 / np.sqrt(R) / fr[:, None], "e2m1")
    wsp = pack_weight(n((K, N)) * 1 / np.sqrt(K) * fk[:, None], "e4m3")
    return {
        "xt_words": xtp[0],
        "xt_scales": xtp[1],
        "w_words": wp[0],
        "w_scales": wp[1],
        "w2_words": w2p[0],
        "w2_scales": w2p[1],
        "wb_words": wbp[0],
        "wb_scales": wbp[1],
        "ws_words": wsp[0],
        "ws_scales": wsp[1],
        "offs": striped(idx),
        "offs2": striped(idx2),
        "offs3": striped(idx3),
        "offs4": striped(idx4),
        "offs5": striped(idx5),
    }


def reference(xt_words, xt_scales, w_words, w_scales, w2_words, w2_scales, wb_words, wb_scales, ws_words, ws_scales, offs, offs2, offs3, offs4, offs5):
    idx = unstriped(offs)
    idx2 = unstriped(offs2)
    idx3 = unstriped(offs3)
    idx4 = unstriped(offs4)
    idx5 = unstriped(offs5)
    xtu = unpack_weight(xt_words, xt_scales, "e2m1")
    wu = unpack_weight(w_words, w_scales, "e4m3")
    w2u = unpack_weight(w2_words, w2_scales, "e5m2")
    wbu = unpack_weight(wb_words, wb_scales, "e2m1")
    wsu = unpack_weight(ws_words, ws_scales, "e4m3")
    xtidxg = xtu[:, idx]
    a = wu.T @ xtidxg
    b = w2u.T @ xtidxg
    pw = np.zeros((R, C))
    pw[:, idx2] = a
    hid = np.maximum(pw[:, idx3], b[:, idx4])
    hidq = mxq(hid, 0, "e5m2")
    xtidx5g = xtu[:, idx5]
    y = wbu.T @ hidq + wsu.T @ xtidx5g
    return y

@@ -1,0 +1,197 @@
+from contextlib import ExitStack
+
+import concourse.mybir as mybir
+
+K, T, J, R, C, O, N = 512, 1024, 256, 512, 512, 128, 256
+P = 128
+PACK = 4
+FLOPS = 2 * (2 * K * R * J + R * N * O + K * N * O)
+
+F32 = mybir.dt.float32
+BF16 = mybir.dt.bfloat16
+I32 = mybir.dt.int32
+U32 = mybir.dt.uint32
+U16 = mybir.dt.uint16
+U8 = mybir.dt.uint8
+E4M3 = mybir.dt.float8_e4m3fn_x4
+E5M2 = mybir.dt.float8_e5m2_x4
+E2M1 = mybir.dt.float4_e2m1fn_x4
+COPY = mybir.ActivationFunctionType.Copy
+MAX = mybir.AluOpType.max
+
+
+def load_scale_rows(nc, plane, scales, quadrants):
+    rows = scales[0].bitcast(I32)
+    for q in quadrants:
+        nc.sync.dma_start(out=plane[32 * q : 32 * q + 4, :].bitcast(I32), in_=rows[4 * q : 4 * q + 4, :])
+
+
+def words_of(packed):
+    return packed[0].rearrange("p n t -> p (n t)").bitcast(I32)
+
+
+def tile_list_postbox_twow_further_plain_kernel(
+    tc, xt_words, xt_scales, w_words, w_scales, w2_words, w2_scales, wb_words, wb_scales,
+    ws_words, ws_scales, offs, offs2, offs3, offs4, offs5, out,
+):
+    nc = tc.nc
+    with ExitStack() as ctx:
+        sb = ctx.enter_context(tc.tile_pool(name="sb", bufs=1))
+        ps = ctx.enter_context(tc.psum_pool(name="ps", bufs=1))
+
+        def tile(name, cols, dtype):
+            return sb.tile([P, cols], dtype, name=name, align_bytes=64)
+
+        l1 = sb.tile([P, J // 16], U16, name="l1")
+        l2 = sb.tile([P, J // 16], U16, name="l2")
+        l3 = sb.tile([P, O // 16], U16, name="l3")
+        l4 = sb.tile([P, O // 16], U16, name="l4")
+        l5 = sb.tile([P, O // 16], U16, name="l5")
+
+        xw = tile("xw", T, U16)
+        xs = tile("xs", T, U8)
+        w_raw = tile("w_raw", R, U32)
+        w_sraw = tile("w_sraw", R, U8)
+        w2_raw = tile("w2_raw", R, U32)
+        w2_sraw = tile("w2_sraw", R, U8)
+        wbw = tile("wbw", 2 * N, U8)
+        wbs = tile("wbs", N, U8)
+        wsw = tile("wsw", N, U32)
+        wss = tile("wss", N, U8)
+
+        for plane in (xs, w_sraw):
+            nc.vector.memset(plane[:].bitcast(I32), 0)
+        for plane in (w2_sraw, wss, wbs):
+            nc.gpsimd.memset(plane[:].bitcast(I32), 0)
+        board = [tile("board%d" % t, C, F32) for t in range(PACK)]
+        for t in range(PACK):
+            nc.gpsimd.memset(board[t][:], 0.0)
+
+        nc.sync.dma_start(l1[:], offs)
+        nc.sync.dma_start(out=w_raw[:].bitcast(I32), in_=words_of(w_words))
+        load_scale_rows(nc, xs, xt_scales, [0])
+        nc.sync.dma_start(out=xw[:].bitcast(I32), in_=xt_words[0].bitcast(I32))
+        load_scale_rows(nc, xs, xt_scales, [1, 2, 3])
+        load_scale_rows(nc, w_sraw, w_scales, range(4))
+        nc.sync.dma_start(l5[:], offs5)
+        nc.sync.dma_start(out=w2_raw[:].bitcast(I32), in_=words_of(w2_words))
+        load_scale_rows(nc, w2_sraw, w2_scales, range(4))
+        nc.sync.dma_start(l2[:], offs2)
+        nc.sync.dma_start(l3[:], offs3)
+        nc.sync.dma_start(l4[:], offs4)
+        nc.sync.dma_start(out=wsw[:].bitcast(I32), in_=words_of(ws_words))
+        load_scale_rows(nc, wss, ws_scales, range(4))
+        nc.sync.dma_start(out=wbw[:].bitcast(I32), in_=wb_words[0].bitcast(I32))
+        load_scale_rows(nc, wbs, wb_scales, range(4))
+
+        def deal(name, raw, dtype, view):
+            dealt = tile(name, R, dtype)
+            nc.vector.tensor_copy(
+                out=dealt[:].bitcast(view).rearrange("p (t m) -> p m t", t=PACK),
+                in_=raw[:].bitcast(view).rearrange("p (m t) -> p m t", t=PACK),
+            )
+            return dealt
+
+        w_codes = deal("w_codes", w_raw, U32, I32)
+        w_plane = deal("w_plane", w_sraw, U8, U8)
+
+        xg_w = tile("xg_w", J, U16)
+        xg_s = tile("xg_s", J, U8)
+        nc.vector.tensor_copy(out=xg_w[:], in_=xw[:].indirect(l1[:]))
+        nc.vector.tensor_copy(out=xg_s[:], in_=xs[:].indirect(l1[:]))
+
+        w2_codes = deal("w2_codes", w2_raw, U32, I32)
+        w2_plane = deal("w2_plane", w2_sraw, U8, U8)
+
+        x5_w = tile("x5_w", O, U16)
+        x5_s = tile("x5_s", O, U8)
+        nc.vector.tensor_copy(out=x5_w[:], in_=xw[:].indirect(l5[:]))
+        nc.vector.tensor_copy(out=x5_s[:], in_=xs[:].indirect(l5[:]))
+
+        a_ps = [ps.tile([P, J], F32, name="a_ps%d" % t) for t in range(PACK)]
+        b_ps = [ps.tile([P, 2, J], F32, name="b_ps%d" % u) for u in range(2)]
+        y_ps = [ps.tile([P, O], F32, name="y_ps%d" % h) for h in range(2)]
+
+        def first_stage(acc, codes, plane, fmt, t):
+            cols = slice(P * t, P * (t + 1))
+            nc.tensor.matmul_mx(
+                out=acc, lhsT=codes[:, cols].bitcast(fmt), lhsT_scale=plane[:, cols],
+                rhs=xg_w[:].bitcast(E2M1), rhs_scale=xg_s[:], start=True, stop=True,
+            )
+
+        for t in range(PACK):
+            first_stage(a_ps[t][:], w_codes, w_plane, E4M3, t)
+        for t in range(PACK):
+            first_stage(b_ps[t // 2][:, t % 2, :], w2_codes, w2_plane, E5M2, t)
+        for h in range(2):
+            cols = slice(P * h, P * (h + 1))
+            nc.tensor.matmul_mx(
+                out=y_ps[h][:], lhsT=wsw[:, cols].bitcast(E4M3), lhsT_scale=wss[:, cols],
+                rhs=x5_w[:].bitcast(E2M1), rhs_scale=x5_s[:], start=True, stop=False,
+            )
+
+        a_sb = [tile("a_sb%d" % t, J, F32) for t in range(PACK)]
+        b_sb = [tile("b_sb%d" % u, 2 * J, F32) for u in range(2)]
+        gp_all = tile("gp_all", PACK * O, F32)
+        gb_all = tile("gb_all", PACK * O, F32)
+
+        for t in range(PACK):
+            nc.scalar.activation(out=a_sb[t][:], in_=a_ps[t][:], func=COPY)
+
+        def scatter(t, on_vector):
+            if on_vector:
+                nc.vector.tensor_copy(out=board[t][:].indirect(l2[:]), in_=a_sb[t][:])
+            else:
+                nc.scalar.activation(out=board[t][:].indirect(l2[:]), in_=a_sb[t][:], func=COPY)
+
+        def gather(dst, window, on_vector):
+            if on_vector:
+                nc.vector.tensor_copy(out=dst, in_=window)
+            else:
+                nc.scalar.activation(out=dst, in_=window, func=COPY)
+
+        def gather_p(t, on_vector):
+            gather(gp_all[:, O * t : O * (t + 1)], board[t][:].indirect(l3[:]), on_vector)
+
+        def gather_b(t, on_vector):
+            window = b_sb[t // 2][:, J * (t % 2) : J * (t % 2 + 1)]
+            gather(gb_all[:, O * t : O * (t + 1)], window.indirect(l4[:]), on_vector)
+
+        scatter(0, True)
+        scatter(2, False)
+        scatter(1, True)
+        for u in range(2):
+            nc.scalar.activation(out=b_sb[u][:], in_=b_ps[u][:].rearrange("p u j -> p (u j)"), func=COPY)
+        scatter(3, False)
+        gather_p(0, True)
+        gather_p(1, True)
+        gather_b(0, True)
+        gather_b(1, True)
+        gather_b(2, True)
+        gather_b(3, True)
+        gather_p(2, False)
+        gather_p(3, False)
+
+        hid = tile("hid", PACK * O, BF16)
+        nc.vector.tensor_tensor(
+            out=hid[:].rearrange("p (c i t) -> p c t i", i=4, t=PACK),
+            in0=gp_all[:].rearrange("p (t c i) -> p c t i", i=4, t=PACK),
+            in1=gb_all[:].rearrange("p (t c i) -> p c t i", i=4, t=PACK),
+            op=MAX,
+        )
+        h_codes = tile("h_codes", O, U32)
+        h_plane = tile("h_plane", O, U8)
+        nc.vector.quantize_mx(out=h_codes[:].bitcast(E5M2), scales=h_plane[:], in_=hid[:])
+
+        for h in range(2):
+            nc.tensor.matmul_mx(
+                out=y_ps[h][:], lhsT=wbw[:, 2 * P * h : 2 * P * (h + 1)].bitcast(E2M1),
+                lhsT_scale=wbs[:, P * h : P * (h + 1)],
+                rhs=h_codes[:].bitcast(E5M2), rhs_scale=h_plane[:], start=False, stop=True,
+            )
+        y0 = tile("y0", O, F32)
+        y1 = tile("y1", O, F32)
+        nc.vector.tensor_copy(out=y0[:], in_=y_ps[0][:])
+        nc.sync.dma_start(out=out[0:P, :], in_=y0[:])
+        nc.scalar.activation(out=y1[:], in_=y_ps[1][:], func=COPY)
+        nc.scalar.dma_start(out=out[P : 2 * P, :], in_=y1[:])

@@ -59,19 +59,16 @@ def tile_list_postbox_twow_further_plain_kernel(
         wsw = tile("wsw", N, U32)
         wss = tile("wss", N, U8)
 
-        for plane in (xs, w_sraw):
+        for plane in (xs, w_sraw, w2_sraw, wss, wbs):
             nc.vector.memset(plane[:].bitcast(I32), 0)
-        for plane in (w2_sraw, wss, wbs):
-            nc.gpsimd.memset(plane[:].bitcast(I32), 0)
         board = [tile("board%d" % t, C, F32) for t in range(PACK)]
         for t in range(PACK):
-            nc.gpsimd.memset(board[t][:], 0.0)
+            nc.vector.memset(board[t][:], 0.0)
 
         nc.sync.dma_start(l1[:], offs)
-        nc.sync.dma_start(out=w_raw[:].bitcast(I32), in_=words_of(w_words))
-        load_scale_rows(nc, xs, xt_scales, [0])
-        nc.sync.dma_start(out=xw[:].bitcast(I32), in_=xt_words[0].bitcast(I32))
-        load_scale_rows(nc, xs, xt_scales, [1, 2, 3])
+        nc.scalar.dma_start(out=xw[:].bitcast(I32), in_=xt_words[0].bitcast(I32))
+        nc.scalar.dma_start(out=w_raw[:].bitcast(I32), in_=words_of(w_words))
+        load_scale_rows(nc, xs, xt_scales, range(4))
         load_scale_rows(nc, w_sraw, w_scales, range(4))
         nc.sync.dma_start(l5[:], offs5)
         nc.sync.dma_start(out=w2_raw[:].bitcast(I32), in_=words_of(w2_words))
@@ -92,13 +89,16 @@ def tile_list_postbox_twow_further_plain_kernel(
             )
             return dealt
 
-        w_codes = deal("w_codes", w_raw, U32, I32)
-        w_plane = deal("w_plane", w_sraw, U8, U8)
-
         xg_w = tile("xg_w", J, U16)
         xg_s = tile("xg_s", J, U8)
         nc.vector.tensor_copy(out=xg_w[:], in_=xw[:].indirect(l1[:]))
         nc.vector.tensor_copy(out=xg_s[:], in_=xs[:].indirect(l1[:]))
+
+        w_codes = deal("w_codes", w_raw, U32, I32)
+        w_plane = tile("w_plane", R, U8)
+        by_slice = w_sraw[:].rearrange("p (m t) -> p t m", t=PACK)
+        nc.vector.tensor_copy(out=w_plane[:, 0:P], in_=by_slice[:, 0, :])
+        nc.vector.tensor_copy(out=w_plane[:, P:].rearrange("p (t m) -> p t m", m=P), in_=by_slice[:, 1:, :])
 
         w2_codes = deal("w2_codes", w2_raw, U32, I32)
         w2_plane = deal("w2_plane", w2_sraw, U8, U8)

@@ -81,11 +81,11 @@ def tile_list_postbox_twow_further_plain_kernel(
         nc.sync.dma_start(out=wbw[:].bitcast(I32), in_=wb_words[0].bitcast(I32))
         load_scale_rows(nc, wbs, wb_scales, range(4))
 
-        def deal(name, raw, dtype, view):
-            dealt = tile(name, R, dtype)
+        def deal_words(name, raw):
+            dealt = tile(name, R, U32)
             nc.vector.tensor_copy(
-                out=dealt[:].bitcast(view).rearrange("p (t m) -> p m t", t=PACK),
-                in_=raw[:].bitcast(view).rearrange("p (m t) -> p m t", t=PACK),
+                out=dealt[:].bitcast(I32).rearrange("p (t c i) -> p c t i", t=PACK, i=4),
+                in_=raw[:].bitcast(I32).rearrange("p (c i t) -> p c t i", t=PACK, i=4),
             )
             return dealt
 
@@ -94,14 +94,18 @@ def tile_list_postbox_twow_further_plain_kernel(
         nc.vector.tensor_copy(out=xg_w[:], in_=xw[:].indirect(l1[:]))
         nc.vector.tensor_copy(out=xg_s[:], in_=xs[:].indirect(l1[:]))
 
-        w_codes = deal("w_codes", w_raw, U32, I32)
+        w_codes = deal_words("w_codes", w_raw)
         w_plane = tile("w_plane", R, U8)
         by_slice = w_sraw[:].rearrange("p (m t) -> p t m", t=PACK)
         nc.vector.tensor_copy(out=w_plane[:, 0:P], in_=by_slice[:, 0, :])
         nc.vector.tensor_copy(out=w_plane[:, P:].rearrange("p (t m) -> p t m", m=P), in_=by_slice[:, 1:, :])
 
-        w2_codes = deal("w2_codes", w2_raw, U32, I32)
-        w2_plane = deal("w2_plane", w2_sraw, U8, U8)
+        w2_codes = deal_words("w2_codes", w2_raw)
+        w2_plane = tile("w2_plane", R, U8)
+        nc.vector.tensor_copy(
+            out=w2_plane[:].rearrange("p (t m) -> p t m", m=P),
+            in_=w2_sraw[:].rearrange("p (m t) -> p t m", t=PACK),
+        )
 
         x5_w = tile("x5_w", O, U16)
         x5_s = tile("x5_s", O, U8)
@@ -135,8 +139,9 @@ def tile_list_postbox_twow_further_plain_kernel(
         gp_all = tile("gp_all", PACK * O, F32)
         gb_all = tile("gb_all", PACK * O, F32)
 
-        for t in range(PACK):
-            nc.scalar.activation(out=a_sb[t][:], in_=a_ps[t][:], func=COPY)
+        nc.scalar.activation(out=a_sb[0][:], in_=a_ps[0][:], func=COPY)
+        for t in range(1, PACK):
+            nc.scalar.copy(out=a_sb[t][:], in_=a_ps[t][:])
 
         def scatter(t, on_vector):
             if on_vector:
@@ -161,7 +166,7 @@ def tile_list_postbox_twow_further_plain_kernel(
         scatter(2, False)
         scatter(1, True)
         for u in range(2):
-            nc.scalar.activation(out=b_sb[u][:], in_=b_ps[u][:].rearrange("p u j -> p (u j)"), func=COPY)
+            nc.scalar.copy(out=b_sb[u][:], in_=b_ps[u][:].rearrange("p u j -> p (u j)"))
         scatter(3, False)
         gather_p(0, True)
         gather_p(1, True)
@@ -193,5 +198,5 @@ def tile_list_postbox_twow_further_plain_kernel(
         y1 = tile("y1", O, F32)
         nc.vector.tensor_copy(out=y0[:], in_=y_ps[0][:])
         nc.sync.dma_start(out=out[0:P, :], in_=y0[:])
-        nc.scalar.activation(out=y1[:], in_=y_ps[1][:], func=COPY)
+        nc.scalar.copy(out=y1[:], in_=y_ps[1][:])
         nc.scalar.dma_start(out=out[P : 2 * P, :], in_=y1[:])

@@ -97,8 +97,11 @@ def tile_list_postbox_twow_further_plain_kernel(
         w_codes = deal_words("w_codes", w_raw)
         w_plane = tile("w_plane", R, U8)
         by_slice = w_sraw[:].rearrange("p (m t) -> p t m", t=PACK)
-        nc.vector.tensor_copy(out=w_plane[:, 0:P], in_=by_slice[:, 0, :])
-        nc.vector.tensor_copy(out=w_plane[:, P:].rearrange("p (t m) -> p t m", m=P), in_=by_slice[:, 1:, :])
+        for u in range(2):
+            nc.vector.tensor_copy(
+                out=w_plane[:, 2 * P * u : 2 * P * (u + 1)].rearrange("p (t m) -> p t m", m=P),
+                in_=by_slice[:, 2 * u : 2 * u + 2, :],
+            )
 
         w2_codes = deal_words("w2_codes", w2_raw)
         w2_plane = tile("w2_plane", R, U8)
@@ -165,17 +168,17 @@ def tile_list_postbox_twow_further_plain_kernel(
         scatter(0, True)
         scatter(2, False)
         scatter(1, True)
-        for u in range(2):
-            nc.scalar.copy(out=b_sb[u][:], in_=b_ps[u][:].rearrange("p u j -> p (u j)"))
         scatter(3, False)
+        nc.scalar.copy(out=b_sb[0][:], in_=b_ps[0][:].rearrange("p u j -> p (u j)"))
+        nc.vector.tensor_copy(out=b_sb[1][:], in_=b_ps[1][:].rearrange("p u j -> p (u j)"))
         gather_p(0, True)
         gather_p(1, True)
-        gather_b(0, True)
-        gather_b(1, True)
+        gather_p(3, False)
+        gather_p(2, True)
         gather_b(2, True)
         gather_b(3, True)
-        gather_p(2, False)
-        gather_p(3, False)
+        gather_b(0, False)
+        gather_b(1, False)
 
         hid = tile("hid", PACK * O, BF16)
         nc.vector.tensor_tensor(

@@ -20,10 +20,10 @@ COPY = mybir.ActivationFunctionType.Copy
 MAX = mybir.AluOpType.max
 
 
-def load_scale_rows(nc, plane, scales, quadrants):
+def load_scale_rows(queue, plane, scales, quadrants):
     rows = scales[0].bitcast(I32)
     for q in quadrants:
-        nc.sync.dma_start(out=plane[32 * q : 32 * q + 4, :].bitcast(I32), in_=rows[4 * q : 4 * q + 4, :])
+        queue.dma_start(out=plane[32 * q : 32 * q + 4, :].bitcast(I32), in_=rows[4 * q : 4 * q + 4, :])
 
 
 def words_of(packed):
@@ -66,20 +66,26 @@ def tile_list_postbox_twow_further_plain_kernel(
             nc.vector.memset(board[t][:], 0.0)
 
         nc.sync.dma_start(l1[:], offs)
-        nc.scalar.dma_start(out=xw[:].bitcast(I32), in_=xt_words[0].bitcast(I32))
-        nc.scalar.dma_start(out=w_raw[:].bitcast(I32), in_=words_of(w_words))
-        load_scale_rows(nc, xs, xt_scales, range(4))
-        load_scale_rows(nc, w_sraw, w_scales, range(4))
+        load_scale_rows(nc.scalar, xs, xt_scales, [0])
+        load_scale_rows(nc.sync, xs, xt_scales, [1])
+        load_scale_rows(nc.scalar, xs, xt_scales, [2])
+        nc.sync.dma_start(out=xw[:].bitcast(I32), in_=xt_words[0].bitcast(I32))
+        load_scale_rows(nc.scalar, xs, xt_scales, [3])
+        nc.sync.dma_start(out=w_raw[:].bitcast(I32), in_=words_of(w_words))
+        load_scale_rows(nc.scalar, w_sraw, w_scales, [0])
+        load_scale_rows(nc.sync, w_sraw, w_scales, [1])
+        load_scale_rows(nc.scalar, w_sraw, w_scales, [2])
+        load_scale_rows(nc.sync, w_sraw, w_scales, [3])
         nc.sync.dma_start(l5[:], offs5)
         nc.sync.dma_start(out=w2_raw[:].bitcast(I32), in_=words_of(w2_words))
-        load_scale_rows(nc, w2_sraw, w2_scales, range(4))
+        load_scale_rows(nc.sync, w2_sraw, w2_scales, [0, 1, 2, 3])
         nc.sync.dma_start(l2[:], offs2)
         nc.sync.dma_start(l3[:], offs3)
         nc.sync.dma_start(l4[:], offs4)
         nc.sync.dma_start(out=wsw[:].bitcast(I32), in_=words_of(ws_words))
-        load_scale_rows(nc, wss, ws_scales, range(4))
+        load_scale_rows(nc.sync, wss, ws_scales, [0, 1, 2, 3])
         nc.sync.dma_start(out=wbw[:].bitcast(I32), in_=wb_words[0].bitcast(I32))
-        load_scale_rows(nc, wbs, wb_scales, range(4))
+        load_scale_rows(nc.sync, wbs, wb_scales, [0, 1, 2, 3])
 
         def deal_words(name, raw):
             dealt = tile(name, R, U32)
@@ -91,8 +97,8 @@ def tile_list_postbox_twow_further_plain_kernel(
 
         xg_w = tile("xg_w", J, U16)
         xg_s = tile("xg_s", J, U8)
-        nc.vector.tensor_copy(out=xg_w[:], in_=xw[:].indirect(l1[:]))
         nc.vector.tensor_copy(out=xg_s[:], in_=xs[:].indirect(l1[:]))
+        nc.vector.tensor_copy(out=xg_w[:], in_=xw[:].indirect(l1[:]))
 
         w_codes = deal_words("w_codes", w_raw)
         w_plane = tile("w_plane", R, U8)

from contextlib import ExitStack

import concourse.mybir as mybir

K, T, J, R, C, O, N = 512, 1024, 256, 512, 512, 128, 256
P = 128
PACK = 4
FLOPS = 2 * (2 * K * R * J + R * N * O + K * N * O)

F32 = mybir.dt.float32
BF16 = mybir.dt.bfloat16
I32 = mybir.dt.int32
U32 = mybir.dt.uint32
U16 = mybir.dt.uint16
U8 = mybir.dt.uint8
E4M3 = mybir.dt.float8_e4m3fn_x4
E5M2 = mybir.dt.float8_e5m2_x4
E2M1 = mybir.dt.float4_e2m1fn_x4
COPY = mybir.ActivationFunctionType.Copy
MAX = mybir.AluOpType.max


def load_scale_rows(queue, plane, scales, quadrants):
    rows = scales[0].bitcast(I32)
    for q in quadrants:
        queue.dma_start(out=plane[32 * q : 32 * q + 4, :].bitcast(I32), in_=rows[4 * q : 4 * q + 4, :])


def words_of(packed):
    return packed[0].rearrange("p n t -> p (n t)").bitcast(I32)


def tile_list_postbox_twow_further_plain_kernel(
    tc, xt_words, xt_scales, w_words, w_scales, w2_words, w2_scales, wb_words, wb_scales,
    ws_words, ws_scales, offs, offs2, offs3, offs4, offs5, out,
):
    nc = tc.nc
    with ExitStack() as ctx:
        sb = ctx.enter_context(tc.tile_pool(name="sb", bufs=1))
        ps = ctx.enter_context(tc.psum_pool(name="ps", bufs=1))

        def tile(name, cols, dtype):
            return sb.tile([P, cols], dtype, name=name, align_bytes=64)

        l1 = sb.tile([P, J // 16], U16, name="l1")
        l2 = sb.tile([P, J // 16], U16, name="l2")
        l3 = sb.tile([P, O // 16], U16, name="l3")
        l4 = sb.tile([P, O // 16], U16, name="l4")
        l5 = sb.tile([P, O // 16], U16, name="l5")

        xw = tile("xw", T, U16)
        xs = tile("xs", T, U8)
        w_raw = tile("w_raw", R, U32)
        w_sraw = tile("w_sraw", R, U8)
        w2_raw = tile("w2_raw", R, U32)
        w2_sraw = tile("w2_sraw", R, U8)
        wbw = tile("wbw", 2 * N, U8)
        wbs = tile("wbs", N, U8)
        wsw = tile("wsw", N, U32)
        wss = tile("wss", N, U8)

        for plane in (xs, w_sraw, w2_sraw, wss, wbs):
            nc.vector.memset(plane[:].bitcast(I32), 0)
        board = [tile("board%d" % t, C, F32) for t in range(PACK)]
        for t in range(PACK):
            nc.vector.memset(board[t][:], 0.0)

        nc.sync.dma_start(l1[:], offs)
        load_scale_rows(nc.scalar, xs, xt_scales, [0])
        load_scale_rows(nc.sync, xs, xt_scales, [1])
        load_scale_rows(nc.scalar, xs, xt_scales, [2])
        nc.sync.dma_start(out=xw[:].bitcast(I32), in_=xt_words[0].bitcast(I32))
        load_scale_rows(nc.scalar, xs, xt_scales, [3])
        nc.sync.dma_start(out=w_raw[:].bitcast(I32), in_=words_of(w_words))
        load_scale_rows(nc.scalar, w_sraw, w_scales, [0])
        load_scale_rows(nc.sync, w_sraw, w_scales, [1])
        load_scale_rows(nc.scalar, w_sraw, w_scales, [2])
        load_scale_rows(nc.sync, w_sraw, w_scales, [3])
        nc.sync.dma_start(l5[:], offs5)
        nc.sync.dma_start(out=w2_raw[:].bitcast(I32), in_=words_of(w2_words))
        load_scale_rows(nc.sync, w2_sraw, w2_scales, [0, 1, 2, 3])
        nc.sync.dma_start(l2[:], offs2)
        nc.sync.dma_start(l3[:], offs3)
        nc.sync.dma_start(l4[:], offs4)
        nc.sync.dma_start(out=wsw[:].bitcast(I32), in_=words_of(ws_words))
        load_scale_rows(nc.sync, wss, ws_scales, [0, 1, 2, 3])
        nc.sync.dma_start(out=wbw[:].bitcast(I32), in_=wb_words[0].bitcast(I32))
        load_scale_rows(nc.sync, wbs, wb_scales, [0, 1, 2, 3])

        def deal_words(name, raw):
            dealt = tile(name, R, U32)
            nc.vector.tensor_copy(
                out=dealt[:].bitcast(I32).rearrange("p (t c i) -> p c t i", t=PACK, i=4),
                in_=raw[:].bitcast(I32).rearrange("p (c i t) -> p c t i", t=PACK, i=4),
            )
            return dealt

        xg_w = tile("xg_w", J, U16)
        xg_s = tile("xg_s", J, U8)
        nc.vector.tensor_copy(out=xg_s[:], in_=xs[:].indirect(l1[:]))
        nc.vector.tensor_copy(out=xg_w[:], in_=xw[:].indirect(l1[:]))

        w_codes = deal_words("w_codes", w_raw)
        w_plane = tile("w_plane", R, U8)
        by_slice = w_sraw[:].rearrange("p (m t) -> p t m", t=PACK)
        for u in range(2):
            nc.vector.tensor_copy(
                out=w_plane[:, 2 * P * u : 2 * P * (u + 1)].rearrange("p (t m) -> p t m", m=P),
                in_=by_slice[:, 2 * u : 2 * u + 2, :],
            )

        w2_codes = deal_words("w2_codes", w2_raw)
        w2_plane = tile("w2_plane", R, U8)
        nc.vector.tensor_copy(
            out=w2_plane[:].rearrange("p (t m) -> p t m", m=P),
            in_=w2_sraw[:].rearrange("p (m t) -> p t m", t=PACK),
        )

        x5_w = tile("x5_w", O, U16)
        x5_s = tile("x5_s", O, U8)
        nc.vector.tensor_copy(out=x5_w[:], in_=xw[:].indirect(l5[:]))
        nc.vector.tensor_copy(out=x5_s[:], in_=xs[:].indirect(l5[:]))

        a_ps = [ps.tile([P, J], F32, name="a_ps%d" % t) for t in range(PACK)]
        b_ps = [ps.tile([P, 2, J], F32, name="b_ps%d" % u) for u in range(2)]
        y_ps = [ps.tile([P, O], F32, name="y_ps%d" % h) for h in range(2)]

        def first_stage(acc, codes, plane, fmt, t):
            cols = slice(P * t, P * (t + 1))
            nc.tensor.matmul_mx(
                out=acc, lhsT=codes[:, cols].bitcast(fmt), lhsT_scale=plane[:, cols],
                rhs=xg_w[:].bitcast(E2M1), rhs_scale=xg_s[:], start=True, stop=True,
            )

        for t in range(PACK):
            first_stage(a_ps[t][:], w_codes, w_plane, E4M3, t)
        for t in range(PACK):
            first_stage(b_ps[t // 2][:, t % 2, :], w2_codes, w2_plane, E5M2, t)
        for h in range(2):
            cols = slice(P * h, P * (h + 1))
            nc.tensor.matmul_mx(
                out=y_ps[h][:], lhsT=wsw[:, cols].bitcast(E4M3), lhsT_scale=wss[:, cols],
                rhs=x5_w[:].bitcast(E2M1), rhs_scale=x5_s[:], start=True, stop=False,
            )

        a_sb = [tile("a_sb%d" % t, J, F32) for t in range(PACK)]
        b_sb = [tile("b_sb%d" % u, 2 * J, F32) for u in range(2)]
        gp_all = tile("gp_all", PACK * O, F32)
        gb_all = tile("gb_all", PACK * O, F32)

        nc.scalar.activation(out=a_sb[0][:], in_=a_ps[0][:], func=COPY)
        for t in range(1, PACK):
            nc.scalar.copy(out=a_sb[t][:], in_=a_ps[t][:])

        def scatter(t, on_vector):
            if on_vector:
                nc.vector.tensor_copy(out=board[t][:].indirect(l2[:]), in_=a_sb[t][:])
            else:
                nc.scalar.activation(out=board[t][:].indirect(l2[:]), in_=a_sb[t][:], func=COPY)

        def gather(dst, window, on_vector):
            if on_vector:
                nc.vector.tensor_copy(out=dst, in_=window)
            else:
                nc.scalar.activation(out=dst, in_=window, func=COPY)

        def gather_p(t, on_vector):
            gather(gp_all[:, O * t : O * (t + 1)], board[t][:].indirect(l3[:]), on_vector)

        def gather_b(t, on_vector):
            window = b_sb[t // 2][:, J * (t % 2) : J * (t % 2 + 1)]
            gather(gb_all[:, O * t : O * (t + 1)], window.indirect(l4[:]), on_vector)

        scatter(0, True)
        scatter(2, False)
        scatter(1, True)
        scatter(3, False)
        nc.scalar.copy(out=b_sb[0][:], in_=b_ps[0][:].rearrange("p u j -> p (u j)"))
        nc.vector.tensor_copy(out=b_sb[1][:], in_=b_ps[1][:].rearrange("p u j -> p (u j)"))
        gather_p(0, True)
        gather_p(1, True)
        gather_p(3, False)
        gather_p(2, True)
        gather_b(2, True)
        gather_b(3, True)
        gather_b(0, False)
        gather_b(1, False)

        hid = tile("hid", PACK * O, BF16)
        nc.vector.tensor_tensor(
            out=hid[:].rearrange("p (c i t) -> p c t i", i=4, t=PACK),
            in0=gp_all[:].rearrange("p (t c i) -> p c t i", i=4, t=PACK),
            in1=gb_all[:].rearrange("p (t c i) -> p c t i", i=4, t=PACK),
            op=MAX,
        )
        h_codes = tile("h_codes", O, U32)
        h_plane = tile("h_plane", O, U8)
        nc.vector.quantize_mx(out=h_codes[:].bitcast(E5M2), scales=h_plane[:], in_=hid[:])

        for h in range(2):
            nc.tensor.matmul_mx(
                out=y_ps[h][:], lhsT=wbw[:, 2 * P * h : 2 * P * (h + 1)].bitcast(E2M1),
                lhsT_scale=wbs[:, P * h : P * (h + 1)],
                rhs=h_codes[:].bitcast(E5M2), rhs_scale=h_plane[:], start=False, stop=True,
            )
        y0 = tile("y0", O, F32)
        y1 = tile("y1", O, F32)
        nc.vector.tensor_copy(out=y0[:], in_=y_ps[0][:])
        nc.sync.dma_start(out=out[0:P, :], in_=y0[:])
        nc.scalar.copy(out=y1[:], in_=y_ps[1][:])
        nc.scalar.dma_start(out=out[P : 2 * P, :], in_=y1[:])
